import numpy as np
import ml_dtypes


def mxq(x, axis, fmt="e4m3"):
    dtype, down = {"e4m3": (ml_dtypes.float8_e4m3fn, 7), "e5m2": (ml_dtypes.float8_e5m2, 14)}[fmt]
    v = np.moveaxis(np.asarray(x, np.float32).astype(ml_dtypes.bfloat16).astype(np.float64), axis, -1)
    blocks = v.reshape(v.shape[:-1] + (-1, 32))
    amax = np.abs(blocks).max(-1, keepdims=True)
    byte = np.maximum(np.where(amax > 0, np.frexp(amax)[1] - 1 + 127, 0) - down, 1)
    scale = np.exp2(byte - 127.0)
    codes = (blocks / scale).astype(np.float32).astype(dtype).astype(np.float64)
    return np.moveaxis((codes * scale).reshape(v.shape), -1, axis)


WIDE = False


def mx_kscale(k):
    if not WIDE:
        return np.ones(k)
    levels = np.array([10, -10, 5, -5, 0])
    if k % 512:
        return np.exp2(np.random.permutation(np.resize(levels, k // 32))).repeat(32)
    a = np.empty((k // 512, 16))
    for p in range(k // 512):
        a[p, :8] = np.random.permutation(np.resize(levels, 8))
        for g in range(8):
            far = levels[np.abs(levels - a[p, g]) >= 10]
            a[p, g + 8] = far[np.random.randint(len(far))]
    return np.exp2(a.ravel()).repeat(32)


def f64(x):
    return np.asarray(x).astype(np.float64)


def striped8(idx):
    return np.asarray(idx).reshape(8, -1, 16).transpose(0, 2, 1).reshape(128, -1).astype(np.uint16)


def unstriped8(offs):
    return offs.reshape(8, 16, -1).transpose(0, 2, 1).reshape(8, -1).astype(np.int64)


def pick8(x, idx, run):
    r = np.arange(len(x))
    return x[r[:, None], idx[r % (8 * run) // run]]


E2M1 = np.array([0.0, 0.5, 1.0, 1.5, 2.0, 3.0, 4.0, 6.0, -0.0, -0.5, -1.0, -1.5, -2.0, -3.0, -4.0, -6.0])


def pack_weight(w, fmt):
    k, n = w.shape
    w = f64(np.asarray(w, np.float32).astype(ml_dtypes.bfloat16)).reshape(k // 32, 32, n)
    amax = np.abs(w).max(1)
    if fmt == "e4m3":
        byte = np.frexp(amax)[1] - 1 + 127 - 7
    else:
        mant, ex = np.frexp(amax / 6.0)
        byte = np.where(mant > 0.5, ex, ex - 1) + 127
    byte = np.clip(np.where(amax > 0, byte, 1), 1, 254)
    scaled = (w * np.exp2(127.0 - byte)[:, None, :]).reshape(k, n).astype(np.float32)
    by_word = np.ascontiguousarray(scaled.reshape(k // 512, 128, 4, n).transpose(0, 1, 3, 2))
    if fmt == "e4m3":
        words = by_word.astype(ml_dtypes.float8_e4m3fn).view(np.uint8)
    else:
        c = by_word.astype(ml_dtypes.float4_e2m1fn).view(np.uint8) & 0xF
        words = (c[..., 0::2] | (c[..., 1::2] << 4)).reshape(k // 512, 128, 2 * n)
    return np.ascontiguousarray(words), np.ascontiguousarray(byte.astype(np.uint8).reshape(k // 512, 16, n))


def unpack_weight(words, scales, fmt):
    g, _, n = scales.shape
    words = np.ascontiguousarray(words).reshape(g, 128, n, -1)
    if fmt == "e4m3":
        vals = words.view(ml_dtypes.float8_e4m3fn).astype(np.float64)
    else:
        nib = np.empty((g, 128, n, 4), np.uint8)
        nib[..., 0::2] = words & 0xF
        nib[..., 1::2] = words >> 4
        vals = E2M1[nib]
    vals = vals * np.repeat(np.exp2(scales.astype(np.float64) - 127.0), 8, axis=1)[..., None]
    return vals.transpose(0, 1, 3, 2).reshape(g * 512, n)


D, T, I, Q = 512, 1024, 512, 128


def setup_inputs():
    n = np.random.standard_normal
    idx = np.stack([np.random.permutation(T)[:I] for _ in range(8)])
    idx2 = np.stack([np.random.permutation(T)[:I] for _ in range(8)])
    idx3 = np.stack([np.random.permutation(T)[:I] for _ in range(8)])
    fd = mx_kscale(D)
    keysp = pack_weight(n((D, T)) / fd[:, None], "e4m3")
    return {
        "query": (n((D, Q)) * 0.9 / np.sqrt(D) * fd[:, None]).astype(np.float32),
        "query2": (n((D, Q)) * 0.9 / np.sqrt(D) * fd[:, None]).astype(np.float32),
        "keys_words": keysp[0],
        "keys_scales": keysp[1],
        "lam": (np.random.uniform(0.5, 1.3, (Q, 1))).astype(np.float32),
        "old": (1.0 * n((Q, T))).astype(np.float32),
        "offs": striped8(idx),
        "offs2": striped8(idx2),
        "offs3": striped8(idx3),
    }


def reference(query, query2, keys_words, keys_scales, lam, old, offs, offs2, offs3):
    idx = unstriped8(offs)
    idx2 = unstriped8(offs2)
    idx3 = unstriped8(offs3)
    keysu = unpack_weight(keys_words, keys_scales, "e4m3")
    queryq = mxq(f64(query), 0, "e4m3")
    a = queryq.T @ keysu
    query2q = mxq(f64(query2), 0, "e4m3")
    b = query2q.T @ keysu
    w = (np.maximum(pick8(a, idx, 16), pick8(b, idx2, 16)) - np.maximum(pick8(a, idx2, 16), pick8(b, idx, 16))) * f64(lam)
    f1 = np.zeros((Q, T))
    f1[np.arange(Q)[:, None], idx3[np.arange(Q) % 128 // 16]] = w
    y = np.maximum(f1, f64(old)) + f64(old) * 0.25
    return y

@@ -1,0 +1,123 @@
+from contextlib import ExitStack
+
+import concourse.mybir as mybir
+
+D, T, SLOTS, Q = 512, 1024, 512, 128
+FLOPS = 2 * 2 * D * Q * T
+
+F32 = mybir.dt.float32
+BF16 = mybir.dt.bfloat16
+I32 = mybir.dt.int32
+U32 = mybir.dt.uint32
+U16 = mybir.dt.uint16
+U8 = mybir.dt.uint8
+FP8X4 = mybir.dt.float8_e4m3fn_x4
+ALU = mybir.AluOpType
+COPY = mybir.ActivationFunctionType.Copy
+
+P = 128
+PACK = 4
+PIECE = 256
+KEY_HALF = 512
+SLOT_PART = 256
+OUT_PART = 256
+
+
+def tile_attend_exchanged_lean_largerput_heads_kernel(
+    tc, query, query2, keys_words, keys_scales, lam, old, offs, offs2, offs3, out
+):
+    nc = tc.nc
+    with ExitStack() as ctx:
+        keep = ctx.enter_context(tc.tile_pool(name="keep", bufs=1))
+        psum = ctx.enter_context(tc.psum_pool(name="psum", bufs=1))
+
+        key_scales = keep.tile([P, T], U8, name="key_scales", align_bytes=64)
+        nc.vector.memset(key_scales[:].bitcast(I32), 0)
+        placed = keep.tile([P, T], F32, name="placed")
+        nc.vector.memset(placed[:], 0.0)
+
+        scale_rows = keys_scales[0].bitcast(I32)
+        for quad in range(4):
+            nc.scalar.dma_start(
+                key_scales[32 * quad : 32 * quad + 4, :].bitcast(I32), scale_rows[4 * quad : 4 * quad + 4, :]
+            )
+
+        word_rows = keys_words[0].rearrange("p c r -> p (c r)").bitcast(I32)
+        raw = [keep.tile([P, PACK, Q], F32, name="raw%d" % s) for s in range(2)]
+        key_words = [keep.tile([P, KEY_HALF], I32, name="key_words%d" % h, align_bytes=64) for h in range(2)]
+        for s, source in enumerate((query, query2)):
+            nc.sync.dma_start(raw[s][:], source.rearrange("(p j) w -> p j w", j=PACK))
+            nc.sync.dma_start(key_words[s][:], word_rows[:, s * KEY_HALF : (s + 1) * KEY_HALF])
+        first = keep.tile([P, SLOTS // 16], U16, name="first")
+        second = keep.tile([P, SLOTS // 16], U16, name="second")
+        places = keep.tile([P, SLOTS // 16], U16, name="places")
+        nc.sync.dma_start(first[:], offs)
+        nc.sync.dma_start(second[:], offs2)
+        nc.sync.dma_start(places[:], offs3)
+        lam_col = keep.tile([P, 1], F32, name="lam_col")
+        nc.sync.dma_start(lam_col[:], lam)
+        old_sb = keep.tile([P, T], F32, name="old_sb")
+        nc.sync.dma_start(old_sb[:], old)
+
+        scores = []
+        for s in range(2):
+            grouped = keep.tile([P, Q, PACK], BF16, name="grouped%d" % s, align_bytes=64)
+            nc.vector.tensor_copy(grouped[:], raw[s][:].rearrange("p j w -> p w j"))
+            codes = keep.tile([P, Q], U32, name="codes%d" % s, align_bytes=64)
+            scales = keep.tile([P, Q], U8, name="scales%d" % s, align_bytes=64)
+            nc.vector.quantize_mx(
+                out=codes[:].bitcast(FP8X4), scales=scales[:], in_=grouped[:].rearrange("p w j -> p (w j)")
+            )
+            score = keep.tile([P, T], F32, name="score%d" % s)
+            for c0 in range(0, T, PIECE):
+                bank = psum.tile([P, PIECE], F32, name="bank%d_%d" % (s, c0))
+                half, within = divmod(c0, KEY_HALF)
+                nc.tensor.matmul_mx(
+                    out=bank[:],
+                    lhsT=codes[:].bitcast(FP8X4),
+                    lhsT_scale=scales[:],
+                    rhs=key_words[half][:, within : within + PIECE].bitcast(FP8X4),
+                    rhs_scale=key_scales[:, c0 : c0 + PIECE],
+                    start=True,
+                    stop=True,
+                )
+                nc.scalar.copy(score[:, c0 : c0 + PIECE], bank[:])
+            scores.append(score)
+        a, b = scores
+
+        cols = SLOT_PART // 16
+        for part in range(SLOTS // SLOT_PART):
+            sl = slice(part * cols, (part + 1) * cols)
+            a1 = keep.tile([P, SLOT_PART], F32, name="a1_%d" % part)
+            a2 = keep.tile([P, SLOT_PART], F32, name="a2_%d" % part)
+            b2 = keep.tile([P, SLOT_PART], F32, name="b2_%d" % part)
+            nb1 = keep.tile([P, SLOT_PART], F32, name="nb1_%d" % part)
+            if part == 0:
+                nc.vector.tensor_copy(a1[:], a[:].indirect(first[:, sl]))
+                nc.vector.tensor_copy(a2[:], a[:].indirect(second[:, sl]))
+                nc.scalar.activation(nb1[:], b[:].indirect(first[:, sl]), COPY, scale=-1.0)
+                nc.vector.tensor_copy(b2[:], b[:].indirect(second[:, sl]))
+            else:
+                nc.scalar.activation(a1[:], a[:].indirect(first[:, sl]), COPY)
+                nc.scalar.activation(b2[:], b[:].indirect(second[:, sl]), COPY)
+                nc.scalar.activation(a2[:], a[:].indirect(second[:, sl]), COPY)
+                nc.scalar.activation(nb1[:], b[:].indirect(first[:, sl]), COPY, scale=-1.0)
+            larger = keep.tile([P, SLOT_PART], F32, name="larger%d" % part)
+            neg_larger = keep.tile([P, SLOT_PART], F32, name="neg_larger%d" % part)
+            nc.vector.scalar_tensor_tensor(neg_larger[:], a2[:], -1.0, nb1[:], ALU.mult, ALU.min)
+            nc.vector.tensor_tensor(larger[:], a1[:], b2[:], ALU.max)
+            nc.vector.tensor_tensor(placed[:].indirect(places[:, sl]), larger[:], neg_larger[:], ALU.add)
+
+        parts = [slice(c0, c0 + OUT_PART) for c0 in range(0, T, OUT_PART)]
+        kept = [keep.tile([P, OUT_PART], F32, name="kept%d" % i) for i in range(len(parts))]
+        done = [keep.tile([P, OUT_PART], F32, name="done%d" % i) for i in range(len(parts))]
+        for i in range(len(parts) + 1):
+            if i < len(parts):
+                nc.vector.scalar_tensor_tensor(
+                    kept[i][:], placed[:, parts[i]], lam_col[:], old_sb[:, parts[i]], ALU.mult, ALU.max
+                )
+            if i > 0:
+                j = i - 1
+                nc.vector.scalar_tensor_tensor(done[j][:], old_sb[:, parts[j]], 0.25, kept[j][:], ALU.mult, ALU.add)
+                queue = nc.sync if j % 2 == 0 else nc.scalar
+                queue.dma_start(out[:, parts[j]], done[j][:])

@@ -17,7 +17,22 @@ COPY = mybir.ActivationFunctionType.Copy
 
 P = 128
 PACK = 4
-PIECE = 256
+PIECES = (
+    (
+        (0, 256, "bank0", False),
+        (256, 256, "bank1", False),
+        (512, 256, "bank2", False),
+        (768, 128, "bank3", True),
+        (896, 128, "bank4", False),
+    ),
+    (
+        (512, 256, "bank5", False),
+        (768, 256, "bank6", False),
+        (0, 256, "bank2", False),
+        (256, 128, "bank3", False),
+        (384, 128, "bank4", False),
+    ),
+)
 KEY_HALF = 512
 SLOT_PART = 256
 OUT_PART = 256
@@ -36,18 +51,19 @@ def tile_attend_exchanged_lean_largerput_heads_kernel(
         placed = keep.tile([P, T], F32, name="placed")
         nc.vector.memset(placed[:], 0.0)
 
-        scale_rows = keys_scales[0].bitcast(I32)
-        for quad in range(4):
-            nc.scalar.dma_start(
-                key_scales[32 * quad : 32 * quad + 4, :].bitcast(I32), scale_rows[4 * quad : 4 * quad + 4, :]
-            )
-
         word_rows = keys_words[0].rearrange("p c r -> p (c r)").bitcast(I32)
         raw = [keep.tile([P, PACK, Q], F32, name="raw%d" % s) for s in range(2)]
         key_words = [keep.tile([P, KEY_HALF], I32, name="key_words%d" % h, align_bytes=64) for h in range(2)]
-        for s, source in enumerate((query, query2)):
-            nc.sync.dma_start(raw[s][:], source.rearrange("(p j) w -> p j w", j=PACK))
-            nc.sync.dma_start(key_words[s][:], word_rows[:, s * KEY_HALF : (s + 1) * KEY_HALF])
+        scale_rows = keys_scales[0].bitcast(I32)
+        nc.sync.dma_start(raw[0][:], query.rearrange("(p j) w -> p j w", j=PACK))
+        nc.sync.dma_start(raw[1][:], query2.rearrange("(p j) w -> p j w", j=PACK))
+        for quad in range(4):
+            queue = nc.sync if quad < 2 else nc.scalar
+            queue.dma_start(
+                key_scales[32 * quad : 32 * quad + 4, :].bitcast(I32), scale_rows[4 * quad : 4 * quad + 4, :]
+            )
+        nc.sync.dma_start(key_words[0][:], word_rows[:, :KEY_HALF])
+        nc.sync.dma_start(key_words[1][:], word_rows[:, KEY_HALF:])
         first = keep.tile([P, SLOTS // 16], U16, name="first")
         second = keep.tile([P, SLOTS // 16], U16, name="second")
         places = keep.tile([P, SLOTS // 16], U16, name="places")
@@ -69,27 +85,30 @@ def tile_attend_exchanged_lean_largerput_heads_kernel(
                 out=codes[:].bitcast(FP8X4), scales=scales[:], in_=grouped[:].rearrange("p w j -> p (w j)")
             )
             score = keep.tile([P, T], F32, name="score%d" % s)
-            for c0 in range(0, T, PIECE):
-                bank = psum.tile([P, PIECE], F32, name="bank%d_%d" % (s, c0))
+            for c0, width, tag, on_vector in PIECES[s]:
+                bank = psum.tile([P, width], F32, name="bank%d_%d" % (s, c0), tag=tag)
                 half, within = divmod(c0, KEY_HALF)
                 nc.tensor.matmul_mx(
                     out=bank[:],
                     lhsT=codes[:].bitcast(FP8X4),
                     lhsT_scale=scales[:],
-                    rhs=key_words[half][:, within : within + PIECE].bitcast(FP8X4),
-                    rhs_scale=key_scales[:, c0 : c0 + PIECE],
+                    rhs=key_words[half][:, within : within + width].bitcast(FP8X4),
+                    rhs_scale=key_scales[:, c0 : c0 + width],
                     start=True,
                     stop=True,
                 )
-                nc.scalar.copy(score[:, c0 : c0 + PIECE], bank[:])
+                if on_vector:
+                    nc.vector.tensor_copy(score[:, c0 : c0 + width], bank[:])
+                else:
+                    nc.scalar.copy(score[:, c0 : c0 + width], bank[:])
             scores.append(score)
         a, b = scores
 
         cols = SLOT_PART // 16
         for part in range(SLOTS // SLOT_PART):
             sl = slice(part * cols, (part + 1) * cols)
-            a1 = keep.tile([P, SLOT_PART], F32, name="a1_%d" % part)
-            a2 = keep.tile([P, SLOT_PART], F32, name="a2_%d" % part)
+            a1 = keep.tile([P, SLOT_PART], F32, name="a1_%d" % part, tag="a1")
+            a2 = keep.tile([P, SLOT_PART], F32, name="a2_%d" % part, tag="a2")
             b2 = keep.tile([P, SLOT_PART], F32, name="b2_%d" % part)
             nb1 = keep.tile([P, SLOT_PART], F32, name="nb1_%d" % part)
             if part == 0:
@@ -98,19 +117,20 @@ def tile_attend_exchanged_lean_largerput_heads_kernel(
                 nc.scalar.activation(nb1[:], b[:].indirect(first[:, sl]), COPY, scale=-1.0)
                 nc.vector.tensor_copy(b2[:], b[:].indirect(second[:, sl]))
             else:
-                nc.scalar.activation(a1[:], a[:].indirect(first[:, sl]), COPY)
-                nc.scalar.activation(b2[:], b[:].indirect(second[:, sl]), COPY)
-                nc.scalar.activation(a2[:], a[:].indirect(second[:, sl]), COPY)
                 nc.scalar.activation(nb1[:], b[:].indirect(first[:, sl]), COPY, scale=-1.0)
+                nc.scalar.activation(a2[:], a[:].indirect(second[:, sl]), COPY)
+                nc.scalar.activation(b2[:], b[:].indirect(second[:, sl]), COPY)
+                nc.scalar.activation(a1[:], a[:].indirect(first[:, sl]), COPY)
             larger = keep.tile([P, SLOT_PART], F32, name="larger%d" % part)
             neg_larger = keep.tile([P, SLOT_PART], F32, name="neg_larger%d" % part)
             nc.vector.scalar_tensor_tensor(neg_larger[:], a2[:], -1.0, nb1[:], ALU.mult, ALU.min)
             nc.vector.tensor_tensor(larger[:], a1[:], b2[:], ALU.max)
             nc.vector.tensor_tensor(placed[:].indirect(places[:, sl]), larger[:], neg_larger[:], ALU.add)
 
-        parts = [slice(c0, c0 + OUT_PART) for c0 in range(0, T, OUT_PART)]
-        kept = [keep.tile([P, OUT_PART], F32, name="kept%d" % i) for i in range(len(parts))]
-        done = [keep.tile([P, OUT_PART], F32, name="done%d" % i) for i in range(len(parts))]
+        edges = (0, 320, 640, 896, 1024)
+        parts = [slice(lo, hi) for lo, hi in zip(edges, edges[1:])]
+        kept = [keep.tile([P, c.stop - c.start], F32, name="kept%d" % i) for i, c in enumerate(parts)]
+        done = [keep.tile([P, c.stop - c.start], F32, name="done%d" % i) for i, c in enumerate(parts)]
         for i in range(len(parts) + 1):
             if i < len(parts):
                 nc.vector.scalar_tensor_tensor(

@@ -53,13 +53,12 @@ def tile_attend_exchanged_lean_largerput_heads_kernel(
 
         word_rows = keys_words[0].rearrange("p c r -> p (c r)").bitcast(I32)
         raw = [keep.tile([P, PACK, Q], F32, name="raw%d" % s) for s in range(2)]
-        key_words = [keep.tile([P, KEY_HALF], I32, name="key_words%d" % h, align_bytes=64) for h in range(2)]
+        key_words = [keep.tile([P, KEY_HALF], I32, name="key_words%d" % h, tag="key_words%d" % h, align_bytes=64) for h in range(2)]
         scale_rows = keys_scales[0].bitcast(I32)
         nc.sync.dma_start(raw[0][:], query.rearrange("(p j) w -> p j w", j=PACK))
         nc.sync.dma_start(raw[1][:], query2.rearrange("(p j) w -> p j w", j=PACK))
         for quad in range(4):
-            queue = nc.sync if quad < 2 else nc.scalar
-            queue.dma_start(
+            nc.sync.dma_start(
                 key_scales[32 * quad : 32 * quad + 4, :].bitcast(I32), scale_rows[4 * quad : 4 * quad + 4, :]
             )
         nc.sync.dma_start(key_words[0][:], word_rows[:, :KEY_HALF])
@@ -105,27 +104,32 @@ def tile_attend_exchanged_lean_largerput_heads_kernel(
         a, b = scores
 
         cols = SLOT_PART // 16
-        for part in range(SLOTS // SLOT_PART):
-            sl = slice(part * cols, (part + 1) * cols)
-            a1 = keep.tile([P, SLOT_PART], F32, name="a1_%d" % part, tag="a1")
-            a2 = keep.tile([P, SLOT_PART], F32, name="a2_%d" % part, tag="a2")
-            b2 = keep.tile([P, SLOT_PART], F32, name="b2_%d" % part)
-            nb1 = keep.tile([P, SLOT_PART], F32, name="nb1_%d" % part)
-            if part == 0:
-                nc.vector.tensor_copy(a1[:], a[:].indirect(first[:, sl]))
-                nc.vector.tensor_copy(a2[:], a[:].indirect(second[:, sl]))
-                nc.scalar.activation(nb1[:], b[:].indirect(first[:, sl]), COPY, scale=-1.0)
-                nc.vector.tensor_copy(b2[:], b[:].indirect(second[:, sl]))
-            else:
-                nc.scalar.activation(nb1[:], b[:].indirect(first[:, sl]), COPY, scale=-1.0)
-                nc.scalar.activation(a2[:], a[:].indirect(second[:, sl]), COPY)
-                nc.scalar.activation(b2[:], b[:].indirect(second[:, sl]), COPY)
-                nc.scalar.activation(a1[:], a[:].indirect(first[:, sl]), COPY)
-            larger = keep.tile([P, SLOT_PART], F32, name="larger%d" % part)
-            neg_larger = keep.tile([P, SLOT_PART], F32, name="neg_larger%d" % part)
-            nc.vector.scalar_tensor_tensor(neg_larger[:], a2[:], -1.0, nb1[:], ALU.mult, ALU.min)
-            nc.vector.tensor_tensor(larger[:], a1[:], b2[:], ALU.max)
-            nc.vector.tensor_tensor(placed[:].indirect(places[:, sl]), larger[:], neg_larger[:], ALU.add)
+        early, late = slice(0, cols), slice(cols, 2 * cols)
+        a1 = keep.tile([P, SLOT_PART], F32, name="a1")
+        a2 = keep.tile([P, SLOT_PART], F32, name="a2")
+        b2 = keep.tile([P, SLOT_PART], F32, name="b2")
+        nb1 = keep.tile([P, SLOT_PART], F32, name="nb1")
+        nc.vector.tensor_copy(a1[:], a[:].indirect(first[:, early]))
+        nc.vector.tensor_copy(a2[:], a[:].indirect(second[:, early]))
+        nc.vector.tensor_copy(b2[:], b[:].indirect(second[:, early]))
+        nc.vector.tensor_scalar(nb1[:], b[:].indirect(first[:, early]), -1.0, 0.0, ALU.mult, ALU.add)
+
+        a_late = keep.tile([P, 2, SLOT_PART], F32, name="a_late", tag="key_words0", align_bytes=64)
+        b2_late = keep.tile([P, SLOT_PART], F32, name="b2_late")
+        nb1_late = keep.tile([P, SLOT_PART], F32, name="nb1_late")
+        nc.scalar.activation(a_late[:, 0, :], a[:].indirect(first[:, late]), COPY)
+        nc.scalar.activation(b2_late[:], b[:].indirect(second[:, late]), COPY)
+        nc.scalar.activation(a_late[:, 1, :], a[:].indirect(second[:, late]), COPY)
+        nc.scalar.activation(nb1_late[:], b[:].indirect(first[:, late]), COPY, scale=-1.0)
+
+        larger = [keep.tile([P, SLOT_PART], F32, name="larger%d" % i) for i in range(2)]
+        neg_larger = [keep.tile([P, SLOT_PART], F32, name="neg_larger%d" % i) for i in range(2)]
+        nc.vector.tensor_tensor(larger[0][:], a1[:], b2[:], ALU.max)
+        nc.vector.scalar_tensor_tensor(neg_larger[0][:], a2[:], -1.0, nb1[:], ALU.mult, ALU.min)
+        nc.vector.tensor_tensor(larger[1][:], a_late[:, 0, :], b2_late[:], ALU.max)
+        nc.vector.tensor_tensor(placed[:].indirect(places[:, early]), larger[0][:], neg_larger[0][:], ALU.add)
+        nc.vector.scalar_tensor_tensor(neg_larger[1][:], a_late[:, 1, :], -1.0, nb1_late[:], ALU.mult, ALU.min)
+        nc.vector.tensor_tensor(placed[:].indirect(places[:, late]), larger[1][:], neg_larger[1][:], ALU.add)
 
         edges = (0, 320, 640, 896, 1024)
         parts = [slice(lo, hi) for lo, hi in zip(edges, edges[1:])]

from contextlib import ExitStack

import concourse.mybir as mybir

D, T, SLOTS, Q = 512, 1024, 512, 128
FLOPS = 2 * 2 * D * Q * T

F32 = mybir.dt.float32
BF16 = mybir.dt.bfloat16
I32 = mybir.dt.int32
U32 = mybir.dt.uint32
U16 = mybir.dt.uint16
U8 = mybir.dt.uint8
FP8X4 = mybir.dt.float8_e4m3fn_x4
ALU = mybir.AluOpType
COPY = mybir.ActivationFunctionType.Copy

P = 128
PACK = 4
PIECES = (
    (
        (0, 256, "bank0", False),
        (256, 256, "bank1", False),
        (512, 256, "bank2", False),
        (768, 128, "bank3", True),
        (896, 128, "bank4", False),
    ),
    (
        (512, 256, "bank5", False),
        (768, 256, "bank6", False),
        (0, 256, "bank2", False),
        (256, 128, "bank3", False),
        (384, 128, "bank4", False),
    ),
)
KEY_HALF = 512
SLOT_PART = 256
OUT_PART = 256


def tile_attend_exchanged_lean_largerput_heads_kernel(
    tc, query, query2, keys_words, keys_scales, lam, old, offs, offs2, offs3, out
):
    nc = tc.nc
    with ExitStack() as ctx:
        keep = ctx.enter_context(tc.tile_pool(name="keep", bufs=1))
        psum = ctx.enter_context(tc.psum_pool(name="psum", bufs=1))

        key_scales = keep.tile([P, T], U8, name="key_scales", align_bytes=64)
        nc.vector.memset(key_scales[:].bitcast(I32), 0)
        placed = keep.tile([P, T], F32, name="placed")
        nc.vector.memset(placed[:], 0.0)

        word_rows = keys_words[0].rearrange("p c r -> p (c r)").bitcast(I32)
        raw = [keep.tile([P, PACK, Q], F32, name="raw%d" % s) for s in range(2)]
        key_words = [keep.tile([P, KEY_HALF], I32, name="key_words%d" % h, tag="key_words%d" % h, align_bytes=64) for h in range(2)]
        scale_rows = keys_scales[0].bitcast(I32)
        nc.sync.dma_start(raw[0][:], query.rearrange("(p j) w -> p j w", j=PACK))
        nc.sync.dma_start(raw[1][:], query2.rearrange("(p j) w -> p j w", j=PACK))
        for quad in range(4):
            nc.sync.dma_start(
                key_scales[32 * quad : 32 * quad + 4, :].bitcast(I32), scale_rows[4 * quad : 4 * quad + 4, :]
            )
        nc.sync.dma_start(key_words[0][:], word_rows[:, :KEY_HALF])
        nc.sync.dma_start(key_words[1][:], word_rows[:, KEY_HALF:])
        first = keep.tile([P, SLOTS // 16], U16, name="first")
        second = keep.tile([P, SLOTS // 16], U16, name="second")
        places = keep.tile([P, SLOTS // 16], U16, name="places")
        nc.sync.dma_start(first[:], offs)
        nc.sync.dma_start(second[:], offs2)
        nc.sync.dma_start(places[:], offs3)
        lam_col = keep.tile([P, 1], F32, name="lam_col")
        nc.sync.dma_start(lam_col[:], lam)
        old_sb = keep.tile([P, T], F32, name="old_sb")
        nc.sync.dma_start(old_sb[:], old)

        scores = []
        for s in range(2):
            grouped = keep.tile([P, Q, PACK], BF16, name="grouped%d" % s, align_bytes=64)
            nc.vector.tensor_copy(grouped[:], raw[s][:].rearrange("p j w -> p w j"))
            codes = keep.tile([P, Q], U32, name="codes%d" % s, align_bytes=64)
            scales = keep.tile([P, Q], U8, name="scales%d" % s, align_bytes=64)
            nc.vector.quantize_mx(
                out=codes[:].bitcast(FP8X4), scales=scales[:], in_=grouped[:].rearrange("p w j -> p (w j)")
            )
            score = keep.tile([P, T], F32, name="score%d" % s)
            for c0, width, tag, on_vector in PIECES[s]:
                bank = psum.tile([P, width], F32, name="bank%d_%d" % (s, c0), tag=tag)
                half, within = divmod(c0, KEY_HALF)
                nc.tensor.matmul_mx(
                    out=bank[:],
                    lhsT=codes[:].bitcast(FP8X4),
                    lhsT_scale=scales[:],
                    rhs=key_words[half][:, within : within + width].bitcast(FP8X4),
                    rhs_scale=key_scales[:, c0 : c0 + width],
                    start=True,
                    stop=True,
                )
                if on_vector:
                    nc.vector.tensor_copy(score[:, c0 : c0 + width], bank[:])
                else:
                    nc.scalar.copy(score[:, c0 : c0 + width], bank[:])
            scores.append(score)
        a, b = scores

        cols = SLOT_PART // 16
        early, late = slice(0, cols), slice(cols, 2 * cols)
        a1 = keep.tile([P, SLOT_PART], F32, name="a1")
        a2 = keep.tile([P, SLOT_PART], F32, name="a2")
        b2 = keep.tile([P, SLOT_PART], F32, name="b2")
        nb1 = keep.tile([P, SLOT_PART], F32, name="nb1")
        nc.vector.tensor_copy(a1[:], a[:].indirect(first[:, early]))
        nc.vector.tensor_copy(a2[:], a[:].indirect(second[:, early]))
        nc.vector.tensor_copy(b2[:], b[:].indirect(second[:, early]))
        nc.vector.tensor_scalar(nb1[:], b[:].indirect(first[:, early]), -1.0, 0.0, ALU.mult, ALU.add)

        a_late = keep.tile([P, 2, SLOT_PART], F32, name="a_late", tag="key_words0", align_bytes=64)
        b2_late = keep.tile([P, SLOT_PART], F32, name="b2_late")
        nb1_late = keep.tile([P, SLOT_PART], F32, name="nb1_late")
        nc.scalar.activation(a_late[:, 0, :], a[:].indirect(first[:, late]), COPY)
        nc.scalar.activation(b2_late[:], b[:].indirect(second[:, late]), COPY)
        nc.scalar.activation(a_late[:, 1, :], a[:].indirect(second[:, late]), COPY)
        nc.scalar.activation(nb1_late[:], b[:].indirect(first[:, late]), COPY, scale=-1.0)

        larger = [keep.tile([P, SLOT_PART], F32, name="larger%d" % i) for i in range(2)]
        neg_larger = [keep.tile([P, SLOT_PART], F32, name="neg_larger%d" % i) for i in range(2)]
        nc.vector.tensor_tensor(larger[0][:], a1[:], b2[:], ALU.max)
        nc.vector.scalar_tensor_tensor(neg_larger[0][:], a2[:], -1.0, nb1[:], ALU.mult, ALU.min)
        nc.vector.tensor_tensor(larger[1][:], a_late[:, 0, :], b2_late[:], ALU.max)
        nc.vector.tensor_tensor(placed[:].indirect(places[:, early]), larger[0][:], neg_larger[0][:], ALU.add)
        nc.vector.scalar_tensor_tensor(neg_larger[1][:], a_late[:, 1, :], -1.0, nb1_late[:], ALU.mult, ALU.min)
        nc.vector.tensor_tensor(placed[:].indirect(places[:, late]), larger[1][:], neg_larger[1][:], ALU.add)

        edges = (0, 320, 640, 896, 1024)
        parts = [slice(lo, hi) for lo, hi in zip(edges, edges[1:])]
        kept = [keep.tile([P, c.stop - c.start], F32, name="kept%d" % i) for i, c in enumerate(parts)]
        done = [keep.tile([P, c.stop - c.start], F32, name="done%d" % i) for i, c in enumerate(parts)]
        for i in range(len(parts) + 1):
            if i < len(parts):
                nc.vector.scalar_tensor_tensor(
                    kept[i][:], placed[:, parts[i]], lam_col[:], old_sb[:, parts[i]], ALU.mult, ALU.max
                )
            if i > 0:
                j = i - 1
                nc.vector.scalar_tensor_tensor(done[j][:], old_sb[:, parts[j]], 0.25, kept[j][:], ALU.mult, ALU.add)
                queue = nc.sync if j % 2 == 0 else nc.scalar
                queue.dma_start(out[:, parts[j]], done[j][:])
